import numpy as np
import ml_dtypes


def mxq(x, axis, fmt="e4m3"):
    dtype, down = {"e4m3": (ml_dtypes.float8_e4m3fn, 7), "e5m2": (ml_dtypes.float8_e5m2, 14)}[fmt]
    v = np.moveaxis(np.asarray(x, np.float32).astype(ml_dtypes.bfloat16).astype(np.float64), axis, -1)
    blocks = v.reshape(v.shape[:-1] + (-1, 32))
    amax = np.abs(blocks).max(-1, keepdims=True)
    byte = np.maximum(np.where(amax > 0, np.frexp(amax)[1] - 1 + 127, 0) - down, 1)
    scale = np.exp2(byte - 127.0)
    codes = (blocks / scale).astype(np.float32).astype(dtype).astype(np.float64)
    return np.moveaxis((codes * scale).reshape(v.shape), -1, axis)


WIDE = False


def mx_kscale(k):
    if not WIDE:
        return np.ones(k)
    levels = np.array([10, -10, 5, -5, 0])
    if k % 512:
        return np.exp2(np.random.permutation(np.resize(levels, k // 32))).repeat(32)
    a = np.empty((k // 512, 16))
    for p in range(k // 512):
        a[p, :8] = np.random.permutation(np.resize(levels, 8))
        for g in range(8):
            far = levels[np.abs(levels - a[p, g]) >= 10]
            a[p, g + 8] = far[np.random.randint(len(far))]
    return np.exp2(a.ravel()).repeat(32)


def f64(x):
    return np.asarray(x).astype(np.float64)


def striped(idx):
    return np.tile(np.asarray(idx).reshape(-1, 16).T, (8, 1)).astype(np.uint16)


def unstriped(offs):
    return offs[:16].T.reshape(-1).astype(np.int64)


E2M1 = np.array([0.0, 0.5, 1.0, 1.5, 2.0, 3.0, 4.0, 6.0, -0.0, -0.5, -1.0, -1.5, -2.0, -3.0, -4.0, -6.0])


def pack_weight(w, fmt):
    k, n = w.shape
    w = f64(np.asarray(w, np.float32).astype(ml_dtypes.bfloat16)).reshape(k // 32, 32, n)
    amax = np.abs(w).max(1)
    if fmt == "e4m3":
        byte = np.frexp(amax)[1] - 1 + 127 - 7
    else:
        mant, ex = np.frexp(amax / 6.0)
        byte = np.where(mant > 0.5, ex, ex - 1) + 127
    byte = np.clip(np.where(amax > 0, byte, 1), 1, 254)
    scaled = (w * np.exp2(127.0 - byte)[:, None, :]).reshape(k, n).astype(np.float32)
    by_word = np.ascontiguousarray(scaled.reshape(k // 512, 128, 4, n).transpose(0, 1, 3, 2))
    if fmt == "e4m3":
        words = by_word.astype(ml_dtypes.float8_e4m3fn).view(np.uint8)
    else:
        c = by_word.astype(ml_dtypes.float4_e2m1fn).view(np.uint8) & 0xF
        words = (c[..., 0::2] | (c[..., 1::2] << 4)).reshape(k // 512, 128, 2 * n)
    return np.ascontiguousarray(words), np.ascontiguousarray(byte.astype(np.uint8).reshape(k // 512, 16, n))


def unpack_weight(words, scales, fmt):
    g, _, n = scales.shape
    words = np.ascontiguousarray(words).reshape(g, 128, n, -1)
    if fmt == "e4m3":
        vals = words.view(ml_dtypes.float8_e4m3fn).astype(np.float64)
    else:
        nib = np.empty((g, 128, n, 4), np.uint8)
        nib[..., 0::2] = words & 0xF
        nib[..., 1::2] = words >> 4
        vals = E2M1[nib]
    vals = vals * np.repeat(np.exp2(scales.astype(np.float64) - 127.0), 8, axis=1)[..., None]
    return vals.transpose(0, 1, 3, 2).reshape(g * 512, n)


D, E, T, I, Q = 512, 512, 2048, 512, 128


def setup_inputs():
    n = np.random.standard_normal
    idx4 = np.random.permutation(I)[:I]
    idx = np.random.permutation(T)[:I]
    fd = mx_kscale(D)
    fe = mx_kscale(E)
    keysp = pack_weight(n((D, T)) / fd[:, None], "e2m1")
    valsp = pack_weight(n((E, T)) / fe[:, None], "e2m1")
    return {
        "query": (n((D, Q)) * 0.8 / np.sqrt(D) * fd[:, None]).astype(np.float32),
        "keys_words": keysp[0],
        "keys_scales": keysp[1],
        "pull": (np.random.uniform(0.4, 1.2, (Q, 1))).astype(np.float32),
        "gout": (n((E, Q)) * 1 / np.sqrt(E) * fe[:, None]).astype(np.float32),
        "vals_words": valsp[0],
        "vals_scales": valsp[1],
        "base": (0.5 * n((Q, I))).astype(np.float32),
        "offs4": striped(idx4),
        "offs": striped(idx),
    }


def reference(query, keys_words, keys_scales, pull, gout, vals_words, vals_scales, base, offs4, offs):
    idx4 = unstriped(offs4)
    idx = unstriped(offs)
    keysu = unpack_weight(keys_words, keys_scales, "e2m1")
    valsu = unpack_weight(vals_words, vals_scales, "e2m1")
    queryq = mxq(f64(query), 0, "e4m3")
    keysidxg = keysu[:, idx]
    a = queryq.T @ keysidxg
    p = np.exp(a - np.max(a, axis=1, keepdims=True))
    goutq = mxq(f64(gout), 0, "e4m3")
    valsidxg = valsu[:, idx]
    c0 = goutq.T @ valsidxg
    e1 = c0 * f64(pull)
    s1 = np.zeros((Q, I))
    s1[:, idx4] = e1
    dr = c0 + s1
    dp = dr / np.sum(p, axis=1, keepdims=True) + np.sum(dr * p / np.square(np.sum(p, axis=1, keepdims=True)) * (-1.0), axis=1, keepdims=True)
    da = dp * p
    hda = da * 512.0 * 2.0 * 512.0
    hdp = hda * p
    hp = hda * dp + np.sum(hdp * dr / np.square(np.sum(p, axis=1, keepdims=True)) * (-1.0), axis=1, keepdims=True) + np.sum(hdp, axis=1, keepdims=True) * (-1.0) / np.square(np.sum(p, axis=1, keepdims=True)) * dr + np.sum(np.sum(hdp, axis=1, keepdims=True) * (-1.0) * dr * p / np.square(np.square(np.sum(p, axis=1, keepdims=True))) * (-1.0), axis=1, keepdims=True) * np.sum(p, axis=1, keepdims=True) * 2.0
    ha = hp * p
    y = ha + f64(base)
    return y

@@ -1,0 +1,164 @@
+import math
+from contextlib import ExitStack
+
+import concourse.mybir as mybir
+
+F32 = mybir.dt.float32
+BF16 = mybir.dt.bfloat16
+I32 = mybir.dt.int32
+U32 = mybir.dt.uint32
+U16 = mybir.dt.uint16
+U8 = mybir.dt.uint8
+FP8X4 = mybir.dt.float8_e4m3fn_x4
+FP4X4 = mybir.dt.float4_e2m1fn_x4
+ALU = mybir.AluOpType
+ACT = mybir.ActivationFunctionType
+AXIS = mybir.AxisListType
+
+P = 128
+PACK = 4
+D, T, SLOTS, Q = 512, 2048, 512, 128
+PENALTY = 512.0 * 2.0 * 512.0
+ROOT = math.sqrt(PENALTY)
+FLOPS = 2 * 2 * D * SLOTS * Q
+HALF = SLOTS // 2
+PER_COLUMN = 16
+
+
+def tile_attend_gpdirect_followed_kernel(tc, query, keys_words, keys_scales, pull, gout, vals_words, vals_scales, base, offs4, offs, out):
+    nc = tc.nc
+    with ExitStack() as ctx:
+        sb = ctx.enter_context(tc.tile_pool(name="sb", bufs=1))
+        shared = ctx.enter_context(tc.tile_pool(name="shared", bufs=1))
+        ps = ctx.enter_context(tc.psum_pool(name="ps", bufs=1))
+
+        token_list = sb.tile([P, SLOTS // PER_COLUMN], U16, name="token_list")
+        slot_list = sb.tile([P, SLOTS // PER_COLUMN], U16, name="slot_list")
+
+        def entries(offsets, part):
+            return offsets[:, part.start // PER_COLUMN : part.stop // PER_COLUMN]
+
+        def load_scales(window, scales, queues):
+            nc.vector.memset(window[:].bitcast(I32), 0)
+            for quad, queue in enumerate(queues):
+                queue.dma_start(out=window[32 * quad : 32 * quad + 4, :].bitcast(I32), in_=scales[0, 4 * quad : 4 * quad + 4, :].bitcast(I32))
+
+        def load_words(name, words):
+            window = sb.tile([P, T], U16, name=name, align_bytes=64)
+            nc.sync.dma_start(out=window[:].bitcast(I32), in_=words[0].bitcast(I32))
+            return window
+
+        def load_rows(name, rows):
+            raw = sb.tile([P, PACK, Q], F32, name=name)
+            nc.sync.dma_start(out=raw[:], in_=rows.rearrange("(p j) q -> p j q", j=PACK))
+            return raw
+
+        def quantise(name, raw, codes):
+            grouped = sb.tile([P, Q, PACK], BF16, name=name + "_bf16", align_bytes=64)
+            nc.scalar.activation(out=grouped[:], in_=raw[:].rearrange("p j q -> p q j"), func=ACT.Copy)
+            scales = sb.tile([P, Q], U8, name=name + "_scales", align_bytes=64)
+            nc.vector.quantize_mx(out=codes[:].bitcast(FP8X4), scales=scales[:], in_=grouped[:].rearrange("p q j -> p (q j)"))
+            return scales
+
+        def gather(picked, window, part):
+            nc.vector.tensor_copy(out=picked, in_=window[:].indirect(entries(token_list, part)))
+
+        def product(name, codes, scales, words, word_scales):
+            bank = ps.tile([P, HALF], F32, name=name)
+            nc.tensor.matmul_mx(out=bank[:], lhsT=codes[:].bitcast(FP8X4), lhsT_scale=scales[:], rhs=words.bitcast(FP4X4), rhs_scale=word_scales, start=True, stop=True)
+            return bank
+
+        def column(name):
+            return sb.tile([P, 1], F32, name=name)
+
+        def wide(name):
+            return sb.tile([P, SLOTS], F32, name=name)
+
+        halves = (slice(0, HALF), slice(HALF, SLOTS))
+        whole = slice(0, SLOTS)
+
+        nc.sync.dma_start(out=token_list[:], in_=offs)
+        vals_scale_window = shared.tile([P, T], U8, name="vals_scale_window", align_bytes=64, offset=0)
+        load_scales(vals_scale_window, vals_scales, (nc.sync, nc.scalar, nc.sync, nc.scalar))
+        gout_raw = load_rows("gout_raw", gout)
+        vals_word_window = load_words("vals_word_window", vals_words)
+        query_raw = load_rows("query_raw", query)
+        pull_col = column("pull_col")
+        nc.sync.dma_start(out=pull_col[:], in_=pull)
+        nc.sync.dma_start(out=slot_list[:], in_=offs4)
+        keys_word_window = load_words("keys_word_window", keys_words)
+        keys_scale_window = sb.tile([P, T], U8, name="keys_scale_window", align_bytes=64)
+        load_scales(keys_scale_window, keys_scales, (nc.sync,) * 4)
+        base_sb = wide("base_sb")
+        nc.sync.dma_start(out=base_sb[:], in_=base)
+
+        vals_picked_scales = sb.tile([P, SLOTS], U8, name="vals_picked_scales", align_bytes=64)
+        gather(vals_picked_scales[:], vals_scale_window, whole)
+        gout_codes = shared.tile([P, Q], U32, name="gout_codes", align_bytes=64, offset=2 * SLOTS)
+        gout_scales = quantise("gout", gout_raw, gout_codes)
+
+        vals_picked = shared.tile([P, SLOTS], U16, name="vals_picked", align_bytes=64, offset=0)
+        s1 = wide("s1")
+        e1 = wide("e1")
+        c0 = []
+        for h, part in enumerate(halves):
+            gather(vals_picked[:, part], vals_word_window, part)
+            c0.append(product("c0_%d" % h, gout_codes, gout_scales, vals_picked[:, part], vals_picked_scales[:, part]))
+            nc.scalar.activation(out=e1[:, part], in_=c0[h][:], func=ACT.Copy, scale=pull_col[:])
+            nc.scalar.activation(out=s1[:].indirect(entries(slot_list, part)), in_=e1[:, part], func=ACT.Copy)
+
+        query_codes = sb.tile([P, Q], U32, name="query_codes", align_bytes=64)
+        query_scales = quantise("query", query_raw, query_codes)
+        keys_picked = sb.tile([P, SLOTS], U16, name="keys_picked", align_bytes=64)
+        gather(keys_picked[:], keys_word_window, whole)
+        keys_picked_scales = sb.tile([P, SLOTS], U8, name="keys_picked_scales", align_bytes=64)
+        neg_score = wide("neg_score")
+        neg_max = None
+        for h, part in enumerate(halves):
+            gather(keys_picked_scales[:, part], keys_scale_window, part)
+            score = product("score_%d" % h, query_codes, query_scales, keys_picked[:, part], keys_picked_scales[:, part])
+            so_far = neg_max
+            neg_max = sb.tile([P, 1], F32, name="neg_max", tag=("neg_max" if h else "dr"))
+            nc.vector.tensor_scalar(out=neg_score[:, part], in0=score[:], scalar1=-1.0, scalar2=(so_far[:] if h else None), op0=ALU.mult, op1=ALU.min, accum_out=neg_max[:])
+
+        p = wide("p")
+        p_sum = column("p_sum")
+        nc.scalar.activation(out=p[:], in_=neg_score[:], func=ACT.Exp, scale=-1.0, bias=neg_max[:], accum_out=p_sum[:])
+
+        dr = wide("dr")
+        for h, part in enumerate(halves):
+            nc.vector.tensor_tensor(out=dr[:, part], in0=c0[h][:], in1=s1[:, part], op=ALU.add)
+        inv = column("inv")
+        nc.vector.reciprocal(out=inv[:], in_=p_sum[:])
+        mean = column("mean")
+        mean_terms = wide("mean_terms")
+        nc.vector.scalar_tensor_tensor(out=mean_terms[:], in0=dr[:], scalar=inv[:], in1=p[:], op0=ALU.mult, op1=ALU.mult, accum_out=mean[:])
+        neg_inv = column("neg_inv")
+        nc.vector.tensor_scalar(out=neg_inv[:], in0=inv[:], scalar1=-1.0, scalar2=None, op0=ALU.mult)
+        root_inv = column("root_inv")
+        nc.vector.tensor_scalar(out=root_inv[:], in0=inv[:], scalar1=ROOT, scalar2=None, op0=ALU.mult)
+        neg_share = wide("neg_share")
+        nc.scalar.activation(out=neg_share[:], in_=p[:], func=ACT.Copy, scale=neg_inv[:])
+        centred = wide("centred")
+        nc.vector.scalar_tensor_tensor(out=centred[:], in0=dr[:], scalar=mean[:], in1=p[:], op0=ALU.subtract, op1=ALU.mult)
+        shift_factor = column("shift_factor")
+        nc.vector.tensor_scalar(out=shift_factor[:], in0=inv[:], scalar1=inv[:], scalar2=-0.5 * ROOT, op0=ALU.mult, op1=ALU.mult)
+
+        shift = column("shift")
+        shift_terms = wide("shift_terms")
+        nc.vector.scalar_tensor_tensor(out=shift_terms[:], in0=centred[:], scalar=shift_factor[:], in1=p[:], op0=ALU.mult, op1=ALU.mult, accum_out=shift[:])
+        energy = column("energy")
+        energy_terms = wide("energy_terms")
+        nc.scalar.activation(out=energy_terms[:], in_=centred[:], func=ACT.Square, scale=root_inv[:], accum_out=energy[:])
+
+        shift_sq = column("shift_sq")
+        nc.vector.tensor_tensor(out=shift_sq[:], in0=shift[:], in1=shift[:], op=ALU.mult)
+        square = wide("square")
+        rest = wide("rest")
+        for part in halves:
+            nc.scalar.activation(out=square[:, part], in_=centred[:, part], func=ACT.Square, scale=root_inv[:], bias=shift[:])
+            nc.vector.scalar_tensor_tensor(out=rest[:, part], in0=neg_share[:, part], scalar=energy[:], in1=base_sb[:, part], op0=ALU.mult, op1=ALU.add)
+        result = wide("result")
+        for part, queue in zip(halves, (nc.sync, nc.scalar)):
+            nc.vector.scalar_tensor_tensor(out=result[:, part], in0=square[:, part], scalar=shift_sq[:], in1=rest[:, part], op0=ALU.subtract, op1=ALU.add)
+            queue.dma_start(out=out[:, part], in_=result[:, part])

@@ -29,7 +29,6 @@ def tile_attend_gpdirect_followed_kernel(tc, query, keys_words, keys_scales, pul
     nc = tc.nc
     with ExitStack() as ctx:
         sb = ctx.enter_context(tc.tile_pool(name="sb", bufs=1))
-        shared = ctx.enter_context(tc.tile_pool(name="shared", bufs=1))
         ps = ctx.enter_context(tc.psum_pool(name="ps", bufs=1))
 
         token_list = sb.tile([P, SLOTS // PER_COLUMN], U16, name="token_list")
@@ -38,9 +37,9 @@ def tile_attend_gpdirect_followed_kernel(tc, query, keys_words, keys_scales, pul
         def entries(offsets, part):
             return offsets[:, part.start // PER_COLUMN : part.stop // PER_COLUMN]
 
-        def load_scales(window, scales, queues):
+        def load_scales(window, scales, queue):
             nc.vector.memset(window[:].bitcast(I32), 0)
-            for quad, queue in enumerate(queues):
+            for quad in range(4):
                 queue.dma_start(out=window[32 * quad : 32 * quad + 4, :].bitcast(I32), in_=scales[0, 4 * quad : 4 * quad + 4, :].bitcast(I32))
 
         def load_words(name, words):
@@ -53,20 +52,19 @@ def tile_attend_gpdirect_followed_kernel(tc, query, keys_words, keys_scales, pul
             nc.sync.dma_start(out=raw[:], in_=rows.rearrange("(p j) q -> p j q", j=PACK))
             return raw
 
-        def quantise(name, raw, codes):
+        def quantise(name, raw, cast):
             grouped = sb.tile([P, Q, PACK], BF16, name=name + "_bf16", align_bytes=64)
-            nc.scalar.activation(out=grouped[:], in_=raw[:].rearrange("p j q -> p q j"), func=ACT.Copy)
+            cast(grouped[:], raw[:].rearrange("p j q -> p q j"))
+            codes = sb.tile([P, Q], U32, name=name + "_codes", align_bytes=64)
             scales = sb.tile([P, Q], U8, name=name + "_scales", align_bytes=64)
             nc.vector.quantize_mx(out=codes[:].bitcast(FP8X4), scales=scales[:], in_=grouped[:].rearrange("p q j -> p (q j)"))
-            return scales
+            return codes, scales
 
         def gather(picked, window, part):
             nc.vector.tensor_copy(out=picked, in_=window[:].indirect(entries(token_list, part)))
 
-        def product(name, codes, scales, words, word_scales):
-            bank = ps.tile([P, HALF], F32, name=name)
-            nc.tensor.matmul_mx(out=bank[:], lhsT=codes[:].bitcast(FP8X4), lhsT_scale=scales[:], rhs=words.bitcast(FP4X4), rhs_scale=word_scales, start=True, stop=True)
-            return bank
+        def product(bank, codes, scales, words, word_scales):
+            nc.tensor.matmul_mx(out=bank, lhsT=codes[:].bitcast(FP8X4), lhsT_scale=scales[:], rhs=words.bitcast(FP4X4), rhs_scale=word_scales, start=True, stop=True)
 
         def column(name):
             return sb.tile([P, 1], F32, name=name)
@@ -78,45 +76,45 @@ def tile_attend_gpdirect_followed_kernel(tc, query, keys_words, keys_scales, pul
         whole = slice(0, SLOTS)
 
         nc.sync.dma_start(out=token_list[:], in_=offs)
-        vals_scale_window = shared.tile([P, T], U8, name="vals_scale_window", align_bytes=64, offset=0)
-        load_scales(vals_scale_window, vals_scales, (nc.sync, nc.scalar, nc.sync, nc.scalar))
+        vals_scale_window = sb.tile([P, T], U8, name="vals_scale_window", align_bytes=64)
+        load_scales(vals_scale_window, vals_scales, nc.scalar)
         gout_raw = load_rows("gout_raw", gout)
         vals_word_window = load_words("vals_word_window", vals_words)
-        query_raw = load_rows("query_raw", query)
         pull_col = column("pull_col")
         nc.sync.dma_start(out=pull_col[:], in_=pull)
-        nc.sync.dma_start(out=slot_list[:], in_=offs4)
+        query_raw = load_rows("query_raw", query)
         keys_word_window = load_words("keys_word_window", keys_words)
+        nc.sync.dma_start(out=slot_list[:], in_=offs4)
         keys_scale_window = sb.tile([P, T], U8, name="keys_scale_window", align_bytes=64)
-        load_scales(keys_scale_window, keys_scales, (nc.sync,) * 4)
+        load_scales(keys_scale_window, keys_scales, nc.sync)
         base_sb = wide("base_sb")
         nc.sync.dma_start(out=base_sb[:], in_=base)
 
-        vals_picked_scales = sb.tile([P, SLOTS], U8, name="vals_picked_scales", align_bytes=64)
-        gather(vals_picked_scales[:], vals_scale_window, whole)
-        gout_codes = shared.tile([P, Q], U32, name="gout_codes", align_bytes=64, offset=2 * SLOTS)
-        gout_scales = quantise("gout", gout_raw, gout_codes)
+        gout_codes, gout_scales = quantise("gout", gout_raw, nc.vector.tensor_copy)
 
-        vals_picked = shared.tile([P, SLOTS], U16, name="vals_picked", align_bytes=64, offset=0)
         s1 = wide("s1")
         e1 = wide("e1")
-        c0 = []
+        c0 = ps.tile([P, SLOTS], F32, name="c0")
         for h, part in enumerate(halves):
-            gather(vals_picked[:, part], vals_word_window, part)
-            c0.append(product("c0_%d" % h, gout_codes, gout_scales, vals_picked[:, part], vals_picked_scales[:, part]))
-            nc.scalar.activation(out=e1[:, part], in_=c0[h][:], func=ACT.Copy, scale=pull_col[:])
+            tag = "vals_scale_window" if h else "vals_picked"
+            vals_picked = sb.tile([P, HALF], U16, name="vals_picked", tag=tag, align_bytes=64)
+            gather(vals_picked[:], vals_word_window, part)
+            vals_picked_scales = sb.tile([P, HALF], U8, name="vals_picked_scales_%d" % h, align_bytes=64)
+            gather(vals_picked_scales[:], vals_scale_window, part)
+            product(c0[:, part], gout_codes, gout_scales, vals_picked[:], vals_picked_scales[:])
+            nc.scalar.activation(out=e1[:, part], in_=c0[:, part], func=ACT.Copy, scale=pull_col[:])
             nc.scalar.activation(out=s1[:].indirect(entries(slot_list, part)), in_=e1[:, part], func=ACT.Copy)
 
-        query_codes = sb.tile([P, Q], U32, name="query_codes", align_bytes=64)
-        query_scales = quantise("query", query_raw, query_codes)
+        query_codes, query_scales = quantise("query", query_raw, lambda dst, src: nc.scalar.activation(out=dst, in_=src, func=ACT.Copy))
         keys_picked = sb.tile([P, SLOTS], U16, name="keys_picked", align_bytes=64)
         gather(keys_picked[:], keys_word_window, whole)
-        keys_picked_scales = sb.tile([P, SLOTS], U8, name="keys_picked_scales", align_bytes=64)
         neg_score = wide("neg_score")
         neg_max = None
         for h, part in enumerate(halves):
-            gather(keys_picked_scales[:, part], keys_scale_window, part)
-            score = product("score_%d" % h, query_codes, query_scales, keys_picked[:, part], keys_picked_scales[:, part])
+            keys_picked_scales = sb.tile([P, HALF], U8, name="keys_picked_scales_%d" % h, align_bytes=64)
+            gather(keys_picked_scales[:], keys_scale_window, part)
+            score = ps.tile([P, HALF], F32, name="score_%d" % h)
+            product(score[:], query_codes, query_scales, keys_picked[:, part], keys_picked_scales[:])
             so_far = neg_max
             neg_max = sb.tile([P, 1], F32, name="neg_max", tag=("neg_max" if h else "dr"))
             nc.vector.tensor_scalar(out=neg_score[:, part], in0=score[:], scalar1=-1.0, scalar2=(so_far[:] if h else None), op0=ALU.mult, op1=ALU.min, accum_out=neg_max[:])
@@ -126,39 +124,32 @@ def tile_attend_gpdirect_followed_kernel(tc, query, keys_words, keys_scales, pul
         nc.scalar.activation(out=p[:], in_=neg_score[:], func=ACT.Exp, scale=-1.0, bias=neg_max[:], accum_out=p_sum[:])
 
         dr = wide("dr")
-        for h, part in enumerate(halves):
-            nc.vector.tensor_tensor(out=dr[:, part], in0=c0[h][:], in1=s1[:, part], op=ALU.add)
+        nc.vector.tensor_tensor(out=dr[:], in0=c0[:], in1=s1[:], op=ALU.add)
         inv = column("inv")
         nc.vector.reciprocal(out=inv[:], in_=p_sum[:])
         mean = column("mean")
         mean_terms = wide("mean_terms")
         nc.vector.scalar_tensor_tensor(out=mean_terms[:], in0=dr[:], scalar=inv[:], in1=p[:], op0=ALU.mult, op1=ALU.mult, accum_out=mean[:])
-        neg_inv = column("neg_inv")
-        nc.vector.tensor_scalar(out=neg_inv[:], in0=inv[:], scalar1=-1.0, scalar2=None, op0=ALU.mult)
-        root_inv = column("root_inv")
-        nc.vector.tensor_scalar(out=root_inv[:], in0=inv[:], scalar1=ROOT, scalar2=None, op0=ALU.mult)
-        neg_share = wide("neg_share")
-        nc.scalar.activation(out=neg_share[:], in_=p[:], func=ACT.Copy, scale=neg_inv[:])
-        centred = wide("centred")
-        nc.vector.scalar_tensor_tensor(out=centred[:], in0=dr[:], scalar=mean[:], in1=p[:], op0=ALU.subtract, op1=ALU.mult)
-        shift_factor = column("shift_factor")
-        nc.vector.tensor_scalar(out=shift_factor[:], in0=inv[:], scalar1=inv[:], scalar2=-0.5 * ROOT, op0=ALU.mult, op1=ALU.mult)
+        share = wide("share")
+        nc.scalar.activation(out=share[:], in_=p[:], func=ACT.Copy, scale=inv[:])
+        da = wide("da")
+        nc.vector.scalar_tensor_tensor(out=da[:], in0=dr[:], scalar=mean[:], in1=share[:], op0=ALU.subtract, op1=ALU.mult)
 
         shift = column("shift")
         shift_terms = wide("shift_terms")
-        nc.vector.scalar_tensor_tensor(out=shift_terms[:], in0=centred[:], scalar=shift_factor[:], in1=p[:], op0=ALU.mult, op1=ALU.mult, accum_out=shift[:])
+        nc.vector.scalar_tensor_tensor(out=shift_terms[:], in0=da[:], scalar=-0.5 * ROOT, in1=share[:], op0=ALU.mult, op1=ALU.mult, accum_out=shift[:])
         energy = column("energy")
         energy_terms = wide("energy_terms")
-        nc.scalar.activation(out=energy_terms[:], in_=centred[:], func=ACT.Square, scale=root_inv[:], accum_out=energy[:])
+        nc.scalar.activation(out=energy_terms[:], in_=da[:], func=ACT.Square, scale=ROOT, accum_out=energy[:])
 
         shift_sq = column("shift_sq")
         nc.vector.tensor_tensor(out=shift_sq[:], in0=shift[:], in1=shift[:], op=ALU.mult)
         square = wide("square")
         rest = wide("rest")
         for part in halves:
-            nc.scalar.activation(out=square[:, part], in_=centred[:, part], func=ACT.Square, scale=root_inv[:], bias=shift[:])
-            nc.vector.scalar_tensor_tensor(out=rest[:, part], in0=neg_share[:, part], scalar=energy[:], in1=base_sb[:, part], op0=ALU.mult, op1=ALU.add)
+            nc.scalar.activation(out=square[:, part], in_=da[:, part], func=ACT.Square, scale=ROOT, bias=shift[:])
+            nc.vector.scalar_tensor_tensor(out=rest[:, part], in0=share[:, part], scalar=energy[:], in1=base_sb[:, part], op0=ALU.mult, op1=ALU.subtract)
         result = wide("result")
         for part, queue in zip(halves, (nc.sync, nc.scalar)):
-            nc.vector.scalar_tensor_tensor(out=result[:, part], in0=square[:, part], scalar=shift_sq[:], in1=rest[:, part], op0=ALU.subtract, op1=ALU.add)
+            nc.vector.scalar_tensor_tensor(out=result[:, part], in0=square[:, part], scalar=shift_sq[:], in1=rest[:, part], op0=ALU.subtract, op1=ALU.subtract)
             queue.dma_start(out=out[:, part], in_=result[:, part])

@@ -54,7 +54,7 @@ def tile_attend_gpdirect_followed_kernel(tc, query, keys_words, keys_scales, pul
 
         def quantise(name, raw, cast):
             grouped = sb.tile([P, Q, PACK], BF16, name=name + "_bf16", align_bytes=64)
-            cast(grouped[:], raw[:].rearrange("p j q -> p q j"))
+            cast(grouped[:].rearrange("p (c i) j -> p c j i", i=4), raw[:].rearrange("p j (c i) -> p c j i", i=4))
             codes = sb.tile([P, Q], U32, name=name + "_codes", align_bytes=64)
             scales = sb.tile([P, Q], U8, name=name + "_scales", align_bytes=64)
             nc.vector.quantize_mx(out=codes[:].bitcast(FP8X4), scales=scales[:], in_=grouped[:].rearrange("p q j -> p (q j)"))
@@ -76,13 +76,13 @@ def tile_attend_gpdirect_followed_kernel(tc, query, keys_words, keys_scales, pul
         whole = slice(0, SLOTS)
 
         nc.sync.dma_start(out=token_list[:], in_=offs)
-        vals_scale_window = sb.tile([P, T], U8, name="vals_scale_window", align_bytes=64)
-        load_scales(vals_scale_window, vals_scales, nc.scalar)
         gout_raw = load_rows("gout_raw", gout)
         vals_word_window = load_words("vals_word_window", vals_words)
+        vals_scale_window = sb.tile([P, T], U8, name="vals_scale_window", align_bytes=64)
+        load_scales(vals_scale_window, vals_scales, nc.sync)
+        query_raw = load_rows("query_raw", query)
         pull_col = column("pull_col")
         nc.sync.dma_start(out=pull_col[:], in_=pull)
-        query_raw = load_rows("query_raw", query)
         keys_word_window = load_words("keys_word_window", keys_words)
         nc.sync.dma_start(out=slot_list[:], in_=offs4)
         keys_scale_window = sb.tile([P, T], U8, name="keys_scale_window", align_bytes=64)

import math
from contextlib import ExitStack

import concourse.mybir as mybir

F32 = mybir.dt.float32
BF16 = mybir.dt.bfloat16
I32 = mybir.dt.int32
U32 = mybir.dt.uint32
U16 = mybir.dt.uint16
U8 = mybir.dt.uint8
FP8X4 = mybir.dt.float8_e4m3fn_x4
FP4X4 = mybir.dt.float4_e2m1fn_x4
ALU = mybir.AluOpType
ACT = mybir.ActivationFunctionType
AXIS = mybir.AxisListType

P = 128
PACK = 4
D, T, SLOTS, Q = 512, 2048, 512, 128
PENALTY = 512.0 * 2.0 * 512.0
ROOT = math.sqrt(PENALTY)
FLOPS = 2 * 2 * D * SLOTS * Q
HALF = SLOTS // 2
PER_COLUMN = 16


def tile_attend_gpdirect_followed_kernel(tc, query, keys_words, keys_scales, pull, gout, vals_words, vals_scales, base, offs4, offs, out):
    nc = tc.nc
    with ExitStack() as ctx:
        sb = ctx.enter_context(tc.tile_pool(name="sb", bufs=1))
        ps = ctx.enter_context(tc.psum_pool(name="ps", bufs=1))

        token_list = sb.tile([P, SLOTS // PER_COLUMN], U16, name="token_list")
        slot_list = sb.tile([P, SLOTS // PER_COLUMN], U16, name="slot_list")

        def entries(offsets, part):
            return offsets[:, part.start // PER_COLUMN : part.stop // PER_COLUMN]

        def load_scales(window, scales, queue):
            nc.vector.memset(window[:].bitcast(I32), 0)
            for quad in range(4):
                queue.dma_start(out=window[32 * quad : 32 * quad + 4, :].bitcast(I32), in_=scales[0, 4 * quad : 4 * quad + 4, :].bitcast(I32))

        def load_words(name, words):
            window = sb.tile([P, T], U16, name=name, align_bytes=64)
            nc.sync.dma_start(out=window[:].bitcast(I32), in_=words[0].bitcast(I32))
            return window

        def load_rows(name, rows):
            raw = sb.tile([P, PACK, Q], F32, name=name)
            nc.sync.dma_start(out=raw[:], in_=rows.rearrange("(p j) q -> p j q", j=PACK))
            return raw

        def quantise(name, raw, cast):
            grouped = sb.tile([P, Q, PACK], BF16, name=name + "_bf16", align_bytes=64)
            cast(grouped[:].rearrange("p (c i) j -> p c j i", i=4), raw[:].rearrange("p j (c i) -> p c j i", i=4))
            codes = sb.tile([P, Q], U32, name=name + "_codes", align_bytes=64)
            scales = sb.tile([P, Q], U8, name=name + "_scales", align_bytes=64)
            nc.vector.quantize_mx(out=codes[:].bitcast(FP8X4), scales=scales[:], in_=grouped[:].rearrange("p q j -> p (q j)"))
            return codes, scales

        def gather(picked, window, part):
            nc.vector.tensor_copy(out=picked, in_=window[:].indirect(entries(token_list, part)))

        def product(bank, codes, scales, words, word_scales):
            nc.tensor.matmul_mx(out=bank, lhsT=codes[:].bitcast(FP8X4), lhsT_scale=scales[:], rhs=words.bitcast(FP4X4), rhs_scale=word_scales, start=True, stop=True)

        def column(name):
            return sb.tile([P, 1], F32, name=name)

        def wide(name):
            return sb.tile([P, SLOTS], F32, name=name)

        halves = (slice(0, HALF), slice(HALF, SLOTS))
        whole = slice(0, SLOTS)

        nc.sync.dma_start(out=token_list[:], in_=offs)
        gout_raw = load_rows("gout_raw", gout)
        vals_word_window = load_words("vals_word_window", vals_words)
        vals_scale_window = sb.tile([P, T], U8, name="vals_scale_window", align_bytes=64)
        load_scales(vals_scale_window, vals_scales, nc.sync)
        query_raw = load_rows("query_raw", query)
        pull_col = column("pull_col")
        nc.sync.dma_start(out=pull_col[:], in_=pull)
        keys_word_window = load_words("keys_word_window", keys_words)
        nc.sync.dma_start(out=slot_list[:], in_=offs4)
        keys_scale_window = sb.tile([P, T], U8, name="keys_scale_window", align_bytes=64)
        load_scales(keys_scale_window, keys_scales, nc.sync)
        base_sb = wide("base_sb")
        nc.sync.dma_start(out=base_sb[:], in_=base)

        gout_codes, gout_scales = quantise("gout", gout_raw, nc.vector.tensor_copy)

        s1 = wide("s1")
        e1 = wide("e1")
        c0 = ps.tile([P, SLOTS], F32, name="c0")
        for h, part in enumerate(halves):
            tag = "vals_scale_window" if h else "vals_picked"
            vals_picked = sb.tile([P, HALF], U16, name="vals_picked", tag=tag, align_bytes=64)
            gather(vals_picked[:], vals_word_window, part)
            vals_picked_scales = sb.tile([P, HALF], U8, name="vals_picked_scales_%d" % h, align_bytes=64)
            gather(vals_picked_scales[:], vals_scale_window, part)
            product(c0[:, part], gout_codes, gout_scales, vals_picked[:], vals_picked_scales[:])
            nc.scalar.activation(out=e1[:, part], in_=c0[:, part], func=ACT.Copy, scale=pull_col[:])
            nc.scalar.activation(out=s1[:].indirect(entries(slot_list, part)), in_=e1[:, part], func=ACT.Copy)

        query_codes, query_scales = quantise("query", query_raw, lambda dst, src: nc.scalar.activation(out=dst, in_=src, func=ACT.Copy))
        keys_picked = sb.tile([P, SLOTS], U16, name="keys_picked", align_bytes=64)
        gather(keys_picked[:], keys_word_window, whole)
        neg_score = wide("neg_score")
        neg_max = None
        for h, part in enumerate(halves):
            keys_picked_scales = sb.tile([P, HALF], U8, name="keys_picked_scales_%d" % h, align_bytes=64)
            gather(keys_picked_scales[:], keys_scale_window, part)
            score = ps.tile([P, HALF], F32, name="score_%d" % h)
            product(score[:], query_codes, query_scales, keys_picked[:, part], keys_picked_scales[:])
            so_far = neg_max
            neg_max = sb.tile([P, 1], F32, name="neg_max", tag=("neg_max" if h else "dr"))
            nc.vector.tensor_scalar(out=neg_score[:, part], in0=score[:], scalar1=-1.0, scalar2=(so_far[:] if h else None), op0=ALU.mult, op1=ALU.min, accum_out=neg_max[:])

        p = wide("p")
        p_sum = column("p_sum")
        nc.scalar.activation(out=p[:], in_=neg_score[:], func=ACT.Exp, scale=-1.0, bias=neg_max[:], accum_out=p_sum[:])

        dr = wide("dr")
        nc.vector.tensor_tensor(out=dr[:], in0=c0[:], in1=s1[:], op=ALU.add)
        inv = column("inv")
        nc.vector.reciprocal(out=inv[:], in_=p_sum[:])
        mean = column("mean")
        mean_terms = wide("mean_terms")
        nc.vector.scalar_tensor_tensor(out=mean_terms[:], in0=dr[:], scalar=inv[:], in1=p[:], op0=ALU.mult, op1=ALU.mult, accum_out=mean[:])
        share = wide("share")
        nc.scalar.activation(out=share[:], in_=p[:], func=ACT.Copy, scale=inv[:])
        da = wide("da")
        nc.vector.scalar_tensor_tensor(out=da[:], in0=dr[:], scalar=mean[:], in1=share[:], op0=ALU.subtract, op1=ALU.mult)

        shift = column("shift")
        shift_terms = wide("shift_terms")
        nc.vector.scalar_tensor_tensor(out=shift_terms[:], in0=da[:], scalar=-0.5 * ROOT, in1=share[:], op0=ALU.mult, op1=ALU.mult, accum_out=shift[:])
        energy = column("energy")
        energy_terms = wide("energy_terms")
        nc.scalar.activation(out=energy_terms[:], in_=da[:], func=ACT.Square, scale=ROOT, accum_out=energy[:])

        shift_sq = column("shift_sq")
        nc.vector.tensor_tensor(out=shift_sq[:], in0=shift[:], in1=shift[:], op=ALU.mult)
        square = wide("square")
        rest = wide("rest")
        for part in halves:
            nc.scalar.activation(out=square[:, part], in_=da[:, part], func=ACT.Square, scale=ROOT, bias=shift[:])
            nc.vector.scalar_tensor_tensor(out=rest[:, part], in0=share[:, part], scalar=energy[:], in1=base_sb[:, part], op0=ALU.mult, op1=ALU.subtract)
        result = wide("result")
        for part, queue in zip(halves, (nc.sync, nc.scalar)):
            nc.vector.scalar_tensor_tensor(out=result[:, part], in0=square[:, part], scalar=shift_sq[:], in1=rest[:, part], op0=ALU.subtract, op1=ALU.subtract)
            queue.dma_start(out=out[:, part], in_=result[:, part])
